import numpy as np
import ml_dtypes


def mxq(x, axis, fmt="e4m3"):
    dtype, down = {"e4m3": (ml_dtypes.float8_e4m3fn, 7), "e5m2": (ml_dtypes.float8_e5m2, 14)}[fmt]
    v = np.moveaxis(np.asarray(x, np.float32).astype(ml_dtypes.bfloat16).astype(np.float64), axis, -1)
    blocks = v.reshape(v.shape[:-1] + (-1, 32))
    amax = np.abs(blocks).max(-1, keepdims=True)
    byte = np.maximum(np.where(amax > 0, np.frexp(amax)[1] - 1 + 127, 0) - down, 1)
    scale = np.exp2(byte - 127.0)
    codes = (blocks / scale).astype(np.float32).astype(dtype).astype(np.float64)
    return np.moveaxis((codes * scale).reshape(v.shape), -1, axis)


WIDE = False


def mx_kscale(k):
    if not WIDE:
        return np.ones(k)
    levels = np.array([18, -18])
    if k % 512:
        return np.exp2(np.random.permutation(np.resize(levels, k // 32))).repeat(32)
    a = np.empty((k // 512, 16))
    for p in range(k // 512):
        a[p, :8] = np.random.permutation(np.resize(levels, 8))
        for g in range(8):
            far = levels[np.abs(levels - a[p, g]) >= 10]
            a[p, g + 8] = far[np.random.randint(len(far))]
    return np.exp2(a.ravel()).repeat(32)


def f64(x):
    return np.asarray(x).astype(np.float64)


def striped(idx):
    return np.tile(np.asarray(idx).reshape(-1, 16).T, (8, 1)).astype(np.uint16)


def unstriped(offs):
    return offs[:16].T.reshape(-1).astype(np.int64)

def planes(y):
    n, m = y.shape
    v = y.astype(np.float32).astype(ml_dtypes.bfloat16).astype(np.float64).reshape(n // 32, 32, m)
    top = np.abs(v).max(1)
    byte = np.clip(np.where(top > 0, np.frexp(top)[1] - 1 + 127 - 7, 1), 1, 254)
    codes = (v * np.exp2(127.0 - byte)[:, None, :]).reshape(n, m).astype(np.float32).astype(ml_dtypes.float8_e4m3fn).view(np.uint8)
    words = codes.reshape(n // 512, 128, 4, m).transpose(0, 1, 3, 2)
    return np.ascontiguousarray(words), np.ascontiguousarray(byte.astype(np.uint8).reshape(n // 512, 16, m))


B, N, T, D, R = 1, 512, 2048, 512, 512


def setup_inputs():
    n = np.random.standard_normal
    idx = np.random.permutation(T)[:B * N]
    s = mx_kscale(D)[:, None]
    u = np.ones(T)
    u[idx] = mx_kscale(B * N)
    r = np.random.uniform(0.5, 2.0, T) * u
    x = n((B, D, R))
    return {
        "xT": (x * s).astype(np.float32),
        "wT": (n((D, T)) * (1.00 / np.sqrt(D)) / s / r).astype(np.float32),
        "y": n((B, R, N)).astype(np.float32),
        "wt": (np.random.uniform(0.5, 1.5, (B, R, 1)) * 1.0 / np.sqrt(R)).astype(np.float32),
        "ts": np.tile(r, (128, 1)).astype(np.float32),
        "offs": striped(idx),
    }


def reference(xT, wT, y, wt, ts, offs):
    idx = unstriped(offs)
    pick = lambda x: x[:, idx].reshape(x.shape[0], B, N).transpose(1, 0, 2)
    w = pick(f64(wT))
    a = mxq(f64(xT), 1, "e4m3").transpose(0, 2, 1) @ mxq(w, 1, "e4m3")
    ts_ = pick(f64(ts))[:, :1, :]
    a = a * ts_
    q = a - f64(y)
    g = f64(wt) * q / (1.0 + q * q)
    g = g * ts_
    gx = mxq(g, 2, "e5m2") @ mxq(w, 2, "e4m3").transpose(0, 2, 1)
    out_0 = gx
    return (out_0,) + planes(out_0[0])

@@ -1,0 +1,202 @@
+from contextlib import ExitStack
+
+import concourse.mybir as mybir
+from concourse.masks import make_identity
+
+N, T, D, R = 512, 2048, 512, 512
+P = 128
+L = 4
+
+FLOPS = 2 * 2 * R * N * D
+BYTES = 4 * (D * R + D * T + R * N + R + T) + 2 * P * N // 16 + 4 * R * D + R * D + R * D // 32
+
+F32 = mybir.dt.float32
+BF16 = mybir.dt.bfloat16
+U32 = mybir.dt.uint32
+I32 = mybir.dt.int32
+U16 = mybir.dt.uint16
+U8 = mybir.dt.uint8
+E4 = mybir.dt.float8_e4m3fn_x4
+E5 = mybir.dt.float8_e5m2_x4
+ALU = mybir.AluOpType
+ACT = mybir.ActivationFunctionType
+
+
+def tile_attend_gcau_pl_x_ts_kernel(tc, xT, wT, y, wt, ts, offs, out_0, out_1, out_2):
+    nc = tc.nc
+    HALF = R // 2
+    with ExitStack() as ctx:
+        sb = ctx.enter_context(tc.tile_pool(name="sb", bufs=1))
+        ps_score = ctx.enter_context(tc.psum_pool(name="ps_score", bufs=1))
+        ps_turn = ctx.enter_context(tc.psum_pool(name="ps_turn", bufs=2))
+        ps_out = ctx.enter_context(tc.psum_pool(name="ps_out", bufs=2))
+
+        def tile(shape, dtype, name):
+            return sb.tile(shape, dtype, name=name, align_bytes=64)
+
+        offsets = sb.tile([P, N // 16], U16, name="offsets")
+        nc.sync.dma_start(offsets[:], offs)
+
+        warm_in = tile([P, 1], F32, "warm_in")
+        warm_out = tile([P, 1], F32, "warm_out")
+        nc.vector.memset(warm_in[:], 1.0)
+        nc.scalar.activation(warm_out[:], warm_in[:], ACT.Abs_reciprocal_sqrt)
+
+        w_rows = wT.rearrange("(p t) c -> p t c", t=L)
+        x_rows = xT[0].rearrange("(p t) r -> p t r", t=L)
+        y_rows = y[0].rearrange("(m j) i -> m j i", j=L)
+        w_plane = [tile([P, T], F32, f"w_plane{t}") for t in range(L)]
+        x_half = [tile([P, L, HALF], F32, f"x_half{u}") for u in range(2)]
+        y_lane = [tile([P, N], F32, f"y_lane{j}") for j in range(L)]
+        wt_cols = tile([P, L], F32, "wt_cols")
+        ts_window = tile([P, T], F32, "ts_window")
+        ts_runs = tile([P, T // P], F32, "ts_runs")
+        nc.scalar.dma_start(ts_runs[:], ts[0].rearrange("(p c) -> p c", p=P))
+        nc.scalar.dma_start(wt_cols[:], wt[0].rearrange("(m j) o -> m (j o)", j=L))
+        for t in range(L):
+            nc.sync.dma_start(w_plane[t][:], w_rows[:, t, :])
+        nc.sync.dma_start(y_lane[0][:], y_rows[:, 0, :])
+        for u in range(2):
+            nc.sync.dma_start(x_half[u][:], x_rows[:, :, u * HALF:(u + 1) * HALF])
+        for j in range(1, L):
+            nc.sync.dma_start(y_lane[j][:], y_rows[:, j, :])
+
+        ident = tile([P, P], F32, "ident")
+        ident_bf = tile([P, P], BF16, "ident_bf")
+        make_identity(nc, ident[:])
+        make_identity(nc, ident_bf[:])
+
+        wg = tile([P, N, L], BF16, "wg")
+        wg_by_slot = wg[:].rearrange("p (r s) t -> p s r t", r=L)
+        ws = tile([P, L, P, L], BF16, "ws")
+        ws_codes = tile([P, D], U32, "ws_codes")
+        ws_scales = tile([P, D], U8, "ws_scales")
+
+        def gather_plane(t):
+            nc.vector.tensor_copy(wg_by_slot[:, :, :, t], w_plane[t][:].indirect(offsets[:]))
+            turned = ps_turn.tile([P, L, P], BF16, name="turn")
+            for r in range(L):
+                nc.tensor.transpose(turned[:, r, :], wg[:, r * P:(r + 1) * P, t], ident_bf[:])
+            nc.scalar.copy(ws[:, t, :, :], turned[:].rearrange("s r p -> s p r"))
+            nc.vector.quantize_mx(
+                out=ws_codes[:, t * P:(t + 1) * P].bitcast(E4),
+                scales=ws_scales[:, t * P:(t + 1) * P],
+                in_=ws[:, t, :, :].rearrange("s p r -> s (p r)"),
+            )
+
+        ts_by_run = ts_window[:].rearrange("q (p c) -> q p c", p=P)
+        for g in range(T // P // L):
+            spread = ps_turn.tile([P, L, P], F32, name="turn")
+            for c in range(L):
+                nc.tensor.transpose(spread[:, c, :], ts_runs[:, L * g + c:L * g + c + 1].to_broadcast([P, P]), ident[:])
+            nc.scalar.copy(ts_by_run[:, :, L * g:L * g + L], spread[:].rearrange("q c p -> q p c"))
+
+        gather_plane(0)
+
+        ts_listed = tile([P, N], F32, "ts_listed")
+        nc.vector.tensor_copy(ts_listed[:], ts_window[:].indirect(offsets[:]))
+        ts_turned = ps_turn.tile([P, L, P], F32, name="turn")
+        for r in range(L):
+            nc.tensor.transpose(ts_turned[:, r, :], ts_listed[:, r:N:L], ident[:])
+        ts_cols = tile([P, L], F32, "ts_cols")
+        nc.scalar.copy(ts_cols[:], ts_turned[:, :, 0])
+        wt_spread = ps_turn.tile([P, L, P], F32, name="turn")
+        for j in range(L):
+            nc.tensor.transpose(wt_spread[:, j, :], wt_cols[:, j:j + 1].to_broadcast([P, P]), ident[:])
+        coef = tile([P, L, L, P], F32, "coef")
+        for r in range(L):
+            nc.scalar.activation(coef[:, :, r, :], wt_spread[:], ACT.Copy, scale=ts_cols[:, r:r + 1])
+
+        for t in range(1, L):
+            gather_plane(t)
+        wg_codes = tile([P, N], U32, "wg_codes")
+        wg_scales = tile([P, N], U8, "wg_scales")
+        nc.vector.quantize_mx(out=wg_codes[:].bitcast(E4), scales=wg_scales[:], in_=wg[:].rearrange("p c t -> p (c t)"))
+
+        y_turned = [tile([P, L, P], F32, f"y_turned{j}") for j in range(L)]
+
+        def turn_y(j):
+            turned = ps_turn.tile([P, L, P], F32, name="turn")
+            for r in range(L):
+                nc.tensor.transpose(turned[:, r, :], y_lane[j][:, r:N:L], ident[:])
+            nc.scalar.copy(y_turned[j][:], turned[:])
+
+        turn_y(0)
+
+        scores = [ps_score.tile([P, R], F32, name=f"score{r}") for r in range(L)]
+        for u in range(2):
+            xg = tile([P, HALF, L], BF16, f"xg{u}")
+            nc.vector.tensor_copy(
+                xg[:].rearrange("p (c i) t -> p c t i", i=4),
+                x_half[u][:].rearrange("p t (c i) -> p c t i", i=4),
+            )
+            x_codes = tile([P, HALF], U32, f"x_codes{u}")
+            x_scales = tile([P, HALF], U8, f"x_scales{u}")
+            nc.vector.quantize_mx(out=x_codes[:].bitcast(E4), scales=x_scales[:], in_=xg[:].rearrange("p c t -> p (c t)"))
+            for r in range(L):
+                nc.tensor.matmul_mx(
+                    scores[r][:, u * HALF:(u + 1) * HALF],
+                    lhsT=wg_codes[:, r * P:(r + 1) * P].bitcast(E4), lhsT_scale=wg_scales[:, r * P:(r + 1) * P],
+                    rhs=x_codes[:].bitcast(E4), rhs_scale=x_scales[:], start=True, stop=True,
+                )
+
+        result = tile([P, L, D], F32, "result")
+        out_rows = out_0[0].rearrange("(m j) d -> m j d", j=L)
+        for j in range(L):
+            if j + 1 < L:
+                turn_y(j + 1)
+            q = tile([P, L, P], F32, f"q{j}")
+            for r in range(L):
+                nc.vector.scalar_tensor_tensor(
+                    q[:, r, :], scores[r][:, j:R:L], ts_cols[:, r:r + 1], y_turned[j][:, r, :], ALU.mult, ALU.subtract,
+                )
+            q_sq = tile([P, L, P], F32, f"q_sq{j}")
+            nc.scalar.activation(q_sq[:], q[:], ACT.Square)
+            root = tile([P, L, P], F32, f"root{j}")
+            nc.scalar.activation(root[:], q_sq[:], ACT.Abs_reciprocal_sqrt, bias=1.0)
+            damp = tile([P, L, P], F32, f"damp{j}")
+            nc.scalar.activation(damp[:], root[:], ACT.Square)
+            qc = tile([P, L, P], F32, f"qc{j}")
+            nc.vector.tensor_tensor(qc[:], q[:], coef[:, j, :, :], ALU.mult)
+            h = tile([P, P, L], BF16, f"h{j}")
+            nc.vector.tensor_tensor(
+                h[:].rearrange("s (c i) r -> s c r i", i=2),
+                qc[:].rearrange("s r (c i) -> s c r i", i=2),
+                damp[:].rearrange("s r (c i) -> s c r i", i=2),
+                ALU.mult,
+            )
+            h_codes = tile([P, P], U32, f"h_codes{j}")
+            h_scales = tile([P, P], U8, f"h_scales{j}")
+            nc.vector.quantize_mx(out=h_codes[:].bitcast(E5), scales=h_scales[:], in_=h[:].rearrange("s m r -> s (m r)"))
+            acc = ps_out.tile([P, D], F32, name="acc")
+            nc.tensor.matmul_mx(
+                acc[:], lhsT=h_codes[:].bitcast(E5), lhsT_scale=h_scales[:],
+                rhs=ws_codes[:].bitcast(E4), rhs_scale=ws_scales[:], start=True, stop=True,
+            )
+            by_feature = acc[:].rearrange("m (t p) -> m p t", t=L)
+            dst = result[:, j, :].rearrange("m (p t) -> m p t", t=L)
+            if j + 1 < L:
+                nc.vector.tensor_copy(dst, by_feature)
+            else:
+                for u in range(2):
+                    nc.scalar.copy(dst[:, u * 64:(u + 1) * 64, :], by_feature[:, u * 64:(u + 1) * 64, :])
+            nc.sync.dma_start(out_rows[:, j, :], result[:, j, :])
+
+        planes = tile([P, D, L], BF16, "planes")
+        out_codes = tile([P, D], U32, "out_codes")
+        out_scales = tile([P, D], U8, "out_scales")
+        words = out_1[0].rearrange("m d j -> m (d j)").bitcast(I32)
+        for u in range(2):
+            cols = slice(u * 256, (u + 1) * 256)
+            nc.vector.tensor_copy(
+                planes[:, cols, :].rearrange("m (c i) j -> m c j i", i=4),
+                result[:, :, cols].rearrange("m j (c i) -> m c j i", i=4),
+            )
+            nc.vector.quantize_mx(
+                out=out_codes[:, cols].bitcast(E4), scales=out_scales[:, cols],
+                in_=planes[:, cols, :].rearrange("m d j -> m (d j)"),
+            )
+            nc.sync.dma_start(words[:, cols], out_codes[:, cols].bitcast(I32))
+        for quad in range(4):
+            eng = nc.scalar if quad % 2 else nc.sync
+            eng.dma_start(out_2[0, 4 * quad:4 * quad + 4, :].bitcast(I32), out_scales[32 * quad:32 * quad + 4, :].bitcast(I32))

@@ -21,177 +21,243 @@ E5 = mybir.dt.float8_e5m2_x4
 ALU = mybir.AluOpType
 ACT = mybir.ActivationFunctionType
 
+X_ROWS_ON_VECTOR = 84
+
 
 def tile_attend_gcau_pl_x_ts_kernel(tc, xT, wT, y, wt, ts, offs, out_0, out_1, out_2):
     nc = tc.nc
-    HALF = R // 2
     with ExitStack() as ctx:
+        lists = ctx.enter_context(tc.tile_pool(name="lists", bufs=1))
         sb = ctx.enter_context(tc.tile_pool(name="sb", bufs=1))
-        ps_score = ctx.enter_context(tc.psum_pool(name="ps_score", bufs=1))
-        ps_turn = ctx.enter_context(tc.psum_pool(name="ps_turn", bufs=2))
-        ps_out = ctx.enter_context(tc.psum_pool(name="ps_out", bufs=2))
+        ps = ctx.enter_context(tc.psum_pool(name="ps", bufs=7))
+        ps_reused = ctx.enter_context(tc.psum_pool(name="ps_reused", bufs=1))
 
-        def tile(shape, dtype, name):
-            return sb.tile(shape, dtype, name=name, align_bytes=64)
+        def tile(shape, dtype, name, tag=None):
+            return sb.tile(shape, dtype, name=name, tag=tag or name, align_bytes=64)
 
-        offsets = sb.tile([P, N // 16], U16, name="offsets")
+        def bank(shape):
+            return ps.tile(shape, F32, name="bank")
+
+        offsets = lists.tile([P, N // 16], U16, name="offsets")
+        w_plane = [tile([P, T], F32, f"w_plane{t}") for t in range(L)]
+        y_rows = y[0].rearrange("(m j) i -> m (j i)", j=L)
+        y_first = tile([P, 2 * N], F32, "y_first")
+        wt_cols = tile([P, L], F32, "wt_cols")
+        ts_runs = tile([P, T // P], F32, "ts_runs")
+        nc.sync.dma_start(ts_runs[:], ts[0].rearrange("(p c) -> p c", p=P))
+        nc.sync.dma_start(y_first[:], y_rows[:, 0:2 * N])
         nc.sync.dma_start(offsets[:], offs)
+        nc.sync.dma_start(wt_cols[:], wt[0].rearrange("(m j) o -> m (j o)", j=L))
+        w_rows = wT.rearrange("(p t) c -> p t c", t=L)
+        for t in range(L):
+            nc.sync.dma_start(w_plane[t][:], w_rows[:, t, :])
 
         warm_in = tile([P, 1], F32, "warm_in")
         warm_out = tile([P, 1], F32, "warm_out")
         nc.vector.memset(warm_in[:], 1.0)
         nc.scalar.activation(warm_out[:], warm_in[:], ACT.Abs_reciprocal_sqrt)
 
-        w_rows = wT.rearrange("(p t) c -> p t c", t=L)
-        x_rows = xT[0].rearrange("(p t) r -> p t r", t=L)
-        y_rows = y[0].rearrange("(m j) i -> m j i", j=L)
-        w_plane = [tile([P, T], F32, f"w_plane{t}") for t in range(L)]
-        x_half = [tile([P, L, HALF], F32, f"x_half{u}") for u in range(2)]
-        y_lane = [tile([P, N], F32, f"y_lane{j}") for j in range(L)]
-        wt_cols = tile([P, L], F32, "wt_cols")
-        ts_window = tile([P, T], F32, "ts_window")
-        ts_runs = tile([P, T // P], F32, "ts_runs")
-        nc.scalar.dma_start(ts_runs[:], ts[0].rearrange("(p c) -> p c", p=P))
-        nc.scalar.dma_start(wt_cols[:], wt[0].rearrange("(m j) o -> m (j o)", j=L))
-        for t in range(L):
-            nc.sync.dma_start(w_plane[t][:], w_rows[:, t, :])
-        nc.sync.dma_start(y_lane[0][:], y_rows[:, 0, :])
-        for u in range(2):
-            nc.sync.dma_start(x_half[u][:], x_rows[:, :, u * HALF:(u + 1) * HALF])
-        for j in range(1, L):
-            nc.sync.dma_start(y_lane[j][:], y_rows[:, j, :])
-
         ident = tile([P, P], F32, "ident")
-        ident_bf = tile([P, P], BF16, "ident_bf")
         make_identity(nc, ident[:])
-        make_identity(nc, ident_bf[:])
 
-        wg = tile([P, N, L], BF16, "wg")
-        wg_by_slot = wg[:].rearrange("p (r s) t -> p s r t", r=L)
-        ws = tile([P, L, P, L], BF16, "ws")
-        ws_codes = tile([P, D], U32, "ws_codes")
-        ws_scales = tile([P, D], U8, "ws_scales")
-
-        def gather_plane(t):
-            nc.vector.tensor_copy(wg_by_slot[:, :, :, t], w_plane[t][:].indirect(offsets[:]))
-            turned = ps_turn.tile([P, L, P], BF16, name="turn")
-            for r in range(L):
-                nc.tensor.transpose(turned[:, r, :], wg[:, r * P:(r + 1) * P, t], ident_bf[:])
-            nc.scalar.copy(ws[:, t, :, :], turned[:].rearrange("s r p -> s p r"))
-            nc.vector.quantize_mx(
-                out=ws_codes[:, t * P:(t + 1) * P].bitcast(E4),
-                scales=ws_scales[:, t * P:(t + 1) * P],
-                in_=ws[:, t, :, :].rearrange("s p r -> s (p r)"),
-            )
-
+        ts_window = tile([P, T], F32, "ts_window")
         ts_by_run = ts_window[:].rearrange("q (p c) -> q p c", p=P)
         for g in range(T // P // L):
-            spread = ps_turn.tile([P, L, P], F32, name="turn")
+            spread = bank([P, L, P])
             for c in range(L):
                 nc.tensor.transpose(spread[:, c, :], ts_runs[:, L * g + c:L * g + c + 1].to_broadcast([P, P]), ident[:])
-            nc.scalar.copy(ts_by_run[:, :, L * g:L * g + L], spread[:].rearrange("q c p -> q p c"))
-
-        gather_plane(0)
+            copy = nc.vector.tensor_copy if g % 2 else nc.scalar.copy
+            copy(ts_by_run[:, :, L * g:L * g + L], spread[:].rearrange("q c p -> q p c"))
 
         ts_listed = tile([P, N], F32, "ts_listed")
         nc.vector.tensor_copy(ts_listed[:], ts_window[:].indirect(offsets[:]))
-        ts_turned = ps_turn.tile([P, L, P], F32, name="turn")
+        ts_turned = bank([P, L, P])
         for r in range(L):
             nc.tensor.transpose(ts_turned[:, r, :], ts_listed[:, r:N:L], ident[:])
         ts_cols = tile([P, L], F32, "ts_cols")
         nc.scalar.copy(ts_cols[:], ts_turned[:, :, 0])
-        wt_spread = ps_turn.tile([P, L, P], F32, name="turn")
+
+        y_turned = [tile([P, L, P], F32, f"y_turned{j}") for j in range(L)]
+
+        def turn_y(j, lane, turned, copy):
+            for r in range(L):
+                nc.tensor.transpose(turned[:, r, :], lane[:, r:N:L], ident[:])
+            copy(y_turned[j][:], turned[:])
+
+        for j in range(2):
+            turn_y(j, y_first[:, j * N:(j + 1) * N], bank([P, L, P]), nc.scalar.copy)
+
+        wt_spread = bank([P, L, P])
         for j in range(L):
             nc.tensor.transpose(wt_spread[:, j, :], wt_cols[:, j:j + 1].to_broadcast([P, P]), ident[:])
         coef = tile([P, L, L, P], F32, "coef")
         for r in range(L):
             nc.scalar.activation(coef[:, :, r, :], wt_spread[:], ACT.Copy, scale=ts_cols[:, r:r + 1])
 
-        for t in range(1, L):
-            gather_plane(t)
+        wg = tile([P, N, L], BF16, "wg", tag="ts_window")
+        wg_by_slot = wg[:].rearrange("p (r s) t -> p s r t", r=L)
+        wg_pairs = wg[:].rearrange("p c t -> p (c t)").bitcast(F32).rearrange("p (c u) -> p c u", u=2)
+        ws_codes = tile([P, D], U32, "ws_codes")
+        ws_scales = tile([P, D], U8, "ws_scales")
+
+        def gather_plane(t):
+            nc.vector.tensor_copy(wg_by_slot[:, :, :, t], w_plane[t][:].indirect(offsets[:]))
+
+        def turn_pair(u):
+            turned = bank([P, L, P])
+            for r in range(L):
+                nc.tensor.transpose(turned[:, r, :], wg_pairs[:, r * P:(r + 1) * P, u], ident[:])
+            return turned
+
+        def quantize_pair(u, turned, tag):
+            ws = tile([P, P, 2, L], BF16, f"ws{u}", tag=tag)
+            halves = turned[:].rearrange("s r p -> s (r p)").bitcast(BF16).rearrange("s (r p e) -> s p e r", r=L, e=2)
+            nc.scalar.copy(ws[:], halves)
+            cols = slice(u * D // 2, (u + 1) * D // 2)
+            nc.vector.quantize_mx(
+                out=ws_codes[:, cols].bitcast(E4), scales=ws_scales[:, cols], in_=ws[:].rearrange("s p e r -> s (p e r)"),
+            )
+
+        gather_plane(0)
+        x_raw = tile([P, L, R], F32, "x_raw", tag="w_plane0")
+        nc.sync.dma_start(x_raw[:], xT[0].rearrange("(p t) r -> p t r", t=L))
+        gather_plane(1)
+        y_lane2 = tile([P, N], F32, "y_lane2", tag="w_plane1")
+        nc.sync.dma_start(y_lane2[:], y_rows[:, 2 * N:3 * N])
+        quantize_pair(0, turn_pair(0), "ws0")
+        gather_plane(2)
+        y_lane3 = tile([P, N], F32, "y_lane3", tag="w_plane2")
+        nc.sync.dma_start(y_lane3[:], y_rows[:, 3 * N:])
+        gather_plane(3)
         wg_codes = tile([P, N], U32, "wg_codes")
         wg_scales = tile([P, N], U8, "wg_scales")
         nc.vector.quantize_mx(out=wg_codes[:].bitcast(E4), scales=wg_scales[:], in_=wg[:].rearrange("p c t -> p (c t)"))
+        turned_pair = turn_pair(1)
 
-        y_turned = [tile([P, L, P], F32, f"y_turned{j}") for j in range(L)]
-
-        def turn_y(j):
-            turned = ps_turn.tile([P, L, P], F32, name="turn")
-            for r in range(L):
-                nc.tensor.transpose(turned[:, r, :], y_lane[j][:, r:N:L], ident[:])
-            nc.scalar.copy(y_turned[j][:], turned[:])
-
-        turn_y(0)
-
-        scores = [ps_score.tile([P, R], F32, name=f"score{r}") for r in range(L)]
-        for u in range(2):
-            xg = tile([P, HALF, L], BF16, f"xg{u}")
-            nc.vector.tensor_copy(
-                xg[:].rearrange("p (c i) t -> p c t i", i=4),
-                x_half[u][:].rearrange("p t (c i) -> p c t i", i=4),
+        xg = tile([P, L, P, L], BF16, "xg", tag="w_plane3")
+        xg_walk = xg[:].rearrange("p j m t -> p m t j")
+        x_walk = x_raw[:].rearrange("p t (m j) -> p m t j", j=L)
+        nc.vector.tensor_copy(xg_walk[:, :X_ROWS_ON_VECTOR], x_walk[:, :X_ROWS_ON_VECTOR])
+        nc.scalar.copy(xg_walk[:, X_ROWS_ON_VECTOR:], x_walk[:, X_ROWS_ON_VECTOR:])
+        turn_y(2, y_lane2[:], bank([P, L, P]), nc.scalar.copy)
+        scores = []
+        for j in range(L):
+            x_codes = tile([P, P], U32, f"x_codes{j}")
+            x_scales = tile([P, P], U8, f"x_scales{j}")
+            nc.vector.quantize_mx(
+                out=x_codes[:].bitcast(E4), scales=x_scales[:], in_=xg[:, j, :, :].rearrange("p m t -> p (m t)"),
             )
-            x_codes = tile([P, HALF], U32, f"x_codes{u}")
-            x_scales = tile([P, HALF], U8, f"x_scales{u}")
-            nc.vector.quantize_mx(out=x_codes[:].bitcast(E4), scales=x_scales[:], in_=xg[:].rearrange("p c t -> p (c t)"))
+            scores.append(ps_reused.tile([P, L, P], F32, name="reused") if j == 0 else bank([P, L, P]))
             for r in range(L):
                 nc.tensor.matmul_mx(
-                    scores[r][:, u * HALF:(u + 1) * HALF],
+                    scores[j][:, r, :],
                     lhsT=wg_codes[:, r * P:(r + 1) * P].bitcast(E4), lhsT_scale=wg_scales[:, r * P:(r + 1) * P],
                     rhs=x_codes[:].bitcast(E4), rhs_scale=x_scales[:], start=True, stop=True,
                 )
+        quantize_pair(1, turned_pair, "w_plane0")
 
         result = tile([P, L, D], F32, "result")
         out_rows = out_0[0].rearrange("(m j) d -> m j d", j=L)
-        for j in range(L):
-            if j + 1 < L:
-                turn_y(j + 1)
-            q = tile([P, L, P], F32, f"q{j}")
+        q = [tile([P, L, P], F32, f"q{j}") for j in range(L)]
+        qc = [tile([P, L, P], F32, f"qc{j}") for j in range(L)]
+        damp = [tile([P, L, P], F32, f"damp{j}") for j in range(L)]
+        q_sq = [tile([P, L, P], F32, f"q_sq{j}") for j in range(L)]
+        root = [tile([P, L, P], F32, f"root{j}") for j in range(L)]
+        h = [tile([P, P, L], BF16, f"h{j}") for j in range(L)]
+        acc = {}
+
+        def residual(j):
             for r in range(L):
                 nc.vector.scalar_tensor_tensor(
-                    q[:, r, :], scores[r][:, j:R:L], ts_cols[:, r:r + 1], y_turned[j][:, r, :], ALU.mult, ALU.subtract,
+                    q[j][:, r, :], scores[j][:, r, :], ts_cols[:, r:r + 1], y_turned[j][:, r, :], ALU.mult, ALU.subtract,
                 )
-            q_sq = tile([P, L, P], F32, f"q_sq{j}")
-            nc.scalar.activation(q_sq[:], q[:], ACT.Square)
-            root = tile([P, L, P], F32, f"root{j}")
-            nc.scalar.activation(root[:], q_sq[:], ACT.Abs_reciprocal_sqrt, bias=1.0)
-            damp = tile([P, L, P], F32, f"damp{j}")
-            nc.scalar.activation(damp[:], root[:], ACT.Square)
-            qc = tile([P, L, P], F32, f"qc{j}")
-            nc.vector.tensor_tensor(qc[:], q[:], coef[:, j, :, :], ALU.mult)
-            h = tile([P, P, L], BF16, f"h{j}")
+
+        def square(j):
+            nc.scalar.activation(q_sq[j][:], q[j][:], ACT.Square)
+
+        def inverse_root(j):
+            nc.scalar.activation(root[j][:], q_sq[j][:], ACT.Abs_reciprocal_sqrt, bias=1.0)
+
+        def damping(j):
+            nc.scalar.activation(damp[j][:], root[j][:], ACT.Square)
+
+        def weigh(j, engine):
+            engine.tensor_tensor(qc[j][:], q[j][:], coef[:, j, :, :], ALU.mult)
+
+        def gradient(j):
             nc.vector.tensor_tensor(
-                h[:].rearrange("s (c i) r -> s c r i", i=2),
-                qc[:].rearrange("s r (c i) -> s c r i", i=2),
-                damp[:].rearrange("s r (c i) -> s c r i", i=2),
+                h[j][:].rearrange("s (c i) r -> s c r i", i=2),
+                qc[j][:].rearrange("s r (c i) -> s c r i", i=2),
+                damp[j][:].rearrange("s r (c i) -> s c r i", i=2),
                 ALU.mult,
             )
+
+        def multiply(j):
             h_codes = tile([P, P], U32, f"h_codes{j}")
             h_scales = tile([P, P], U8, f"h_scales{j}")
-            nc.vector.quantize_mx(out=h_codes[:].bitcast(E5), scales=h_scales[:], in_=h[:].rearrange("s m r -> s (m r)"))
-            acc = ps_out.tile([P, D], F32, name="acc")
+            nc.vector.quantize_mx(out=h_codes[:].bitcast(E5), scales=h_scales[:], in_=h[j][:].rearrange("s m r -> s (m r)"))
+            acc[j] = bank([P, D])
             nc.tensor.matmul_mx(
-                acc[:], lhsT=h_codes[:].bitcast(E5), lhsT_scale=h_scales[:],
+                acc[j][:], lhsT=h_codes[:].bitcast(E5), lhsT_scale=h_scales[:],
                 rhs=ws_codes[:].bitcast(E4), rhs_scale=ws_scales[:], start=True, stop=True,
             )
-            by_feature = acc[:].rearrange("m (t p) -> m p t", t=L)
-            dst = result[:, j, :].rearrange("m (p t) -> m p t", t=L)
-            if j + 1 < L:
-                nc.vector.tensor_copy(dst, by_feature)
-            else:
-                for u in range(2):
-                    nc.scalar.copy(dst[:, u * 64:(u + 1) * 64, :], by_feature[:, u * 64:(u + 1) * 64, :])
+
+        def emit(j, parts):
+            by_feature = acc[j][:].rearrange("m (u p e) -> m p u e", u=2, e=2)
+            dst = result[:, j, :].rearrange("m (p u e) -> m p u e", u=2, e=2)
+            step = P // parts
+            for part in range(parts):
+                nc.scalar.copy(dst[:, part * step:(part + 1) * step], by_feature[:, part * step:(part + 1) * step])
             nc.sync.dma_start(out_rows[:, j, :], result[:, j, :])
 
         planes = tile([P, D, L], BF16, "planes")
         out_codes = tile([P, D], U32, "out_codes")
         out_scales = tile([P, D], U8, "out_scales")
         words = out_1[0].rearrange("m d j -> m (d j)").bitcast(I32)
-        for u in range(2):
-            cols = slice(u * 256, (u + 1) * 256)
+
+        def weave(lanes, cols):
             nc.vector.tensor_copy(
-                planes[:, cols, :].rearrange("m (c i) j -> m c j i", i=4),
-                result[:, :, cols].rearrange("m j (c i) -> m c j i", i=4),
+                planes[:, cols, lanes].rearrange("m (c i) j -> m c j i", i=4),
+                result[:, lanes, cols].rearrange("m j (c i) -> m c j i", i=4),
             )
+
+        for j in range(L - 1):
+            residual(j)
+        weigh(0, nc.gpsimd)
+        weigh(1, nc.gpsimd)
+        turn_y(3, y_lane3[:], ps_reused.tile([P, L, P], F32, name="reused"), nc.vector.tensor_copy)
+
+        residual(3)
+        square(0)
+        square(1)
+        inverse_root(0)
+        square(2)
+        inverse_root(1)
+        damping(0)
+        inverse_root(2)
+        damping(1)
+        square(3)
+        damping(2)
+        inverse_root(3)
+        damping(3)
+        gradient(0)
+        weigh(2, nc.vector)
+        multiply(0)
+        gradient(1)
+        weigh(3, nc.vector)
+        multiply(1)
+        gradient(2)
+        multiply(2)
+        gradient(3)
+        multiply(3)
+        for j in range(L - 1):
+            emit(j, 1)
+        weave(slice(0, 2), slice(0, D))
+        emit(3, 2)
+        halves = [slice(0, D // 2), slice(D // 2, D)]
+        for cols in halves:
+            weave(slice(2, 4), cols)
+        for cols in halves:
             nc.vector.quantize_mx(
                 out=out_codes[:, cols].bitcast(E4), scales=out_scales[:, cols],
                 in_=planes[:, cols, :].rearrange("m d j -> m (d j)"),

@@ -21,36 +21,38 @@ E5 = mybir.dt.float8_e5m2_x4
 ALU = mybir.AluOpType
 ACT = mybir.ActivationFunctionType
 
-X_ROWS_ON_VECTOR = 84
-
 
 def tile_attend_gcau_pl_x_ts_kernel(tc, xT, wT, y, wt, ts, offs, out_0, out_1, out_2):
     nc = tc.nc
     with ExitStack() as ctx:
         lists = ctx.enter_context(tc.tile_pool(name="lists", bufs=1))
         sb = ctx.enter_context(tc.tile_pool(name="sb", bufs=1))
-        ps = ctx.enter_context(tc.psum_pool(name="ps", bufs=7))
-        ps_reused = ctx.enter_context(tc.psum_pool(name="ps_reused", bufs=1))
+        ps = ctx.enter_context(tc.psum_pool(name="ps", bufs=1))
 
         def tile(shape, dtype, name, tag=None):
             return sb.tile(shape, dtype, name=name, tag=tag or name, align_bytes=64)
 
-        def bank(shape):
-            return ps.tile(shape, F32, name="bank")
+        def bank(b, shape, dtype=F32):
+            return ps.tile(shape, dtype, name=f"bank{b}", tag=f"bank{b}")
+
+        y_rows = y[0].rearrange("(m j) i -> m j i", j=L)
+        w_rows = wT.rearrange("(p t) c -> p t c", t=L)
 
         offsets = lists.tile([P, N // 16], U16, name="offsets")
-        w_plane = [tile([P, T], F32, f"w_plane{t}") for t in range(L)]
-        y_rows = y[0].rearrange("(m j) i -> m (j i)", j=L)
-        y_first = tile([P, 2 * N], F32, "y_first")
         wt_cols = tile([P, L], F32, "wt_cols")
         ts_runs = tile([P, T // P], F32, "ts_runs")
+        x_raw = tile([P, L, R], F32, "x_raw")
+        y_lane = [tile([P, N], F32, f"y_lane{j}") for j in range(L)]
+        w_plane = [tile([P, T], F32, f"w_plane{t}") for t in range(L)]
         nc.sync.dma_start(ts_runs[:], ts[0].rearrange("(p c) -> p c", p=P))
-        nc.sync.dma_start(y_first[:], y_rows[:, 0:2 * N])
+        nc.sync.dma_start(y_lane[0][:], y_rows[:, 0, :])
         nc.sync.dma_start(offsets[:], offs)
         nc.sync.dma_start(wt_cols[:], wt[0].rearrange("(m j) o -> m (j o)", j=L))
-        w_rows = wT.rearrange("(p t) c -> p t c", t=L)
         for t in range(L):
             nc.sync.dma_start(w_plane[t][:], w_rows[:, t, :])
+        nc.sync.dma_start(x_raw[:], xT[0].rearrange("(p t) r -> p t r", t=L))
+        for j in range(1, L):
+            nc.sync.dma_start(y_lane[j][:], y_rows[:, j, :])
 
         warm_in = tile([P, 1], F32, "warm_in")
         warm_out = tile([P, 1], F32, "warm_out")
@@ -59,11 +61,13 @@ def tile_attend_gcau_pl_x_ts_kernel(tc, xT, wT, y, wt, ts, offs, out_0, out_1, o
 
         ident = tile([P, P], F32, "ident")
         make_identity(nc, ident[:])
+        ident_bf = tile([P, P], BF16, "ident_bf")
+        make_identity(nc, ident_bf[:])
 
         ts_window = tile([P, T], F32, "ts_window")
         ts_by_run = ts_window[:].rearrange("q (p c) -> q p c", p=P)
         for g in range(T // P // L):
-            spread = bank([P, L, P])
+            spread = bank(g, [P, L, P])
             for c in range(L):
                 nc.tensor.transpose(spread[:, c, :], ts_runs[:, L * g + c:L * g + c + 1].to_broadcast([P, P]), ident[:])
             copy = nc.vector.tensor_copy if g % 2 else nc.scalar.copy
@@ -71,7 +75,8 @@ def tile_attend_gcau_pl_x_ts_kernel(tc, xT, wT, y, wt, ts, offs, out_0, out_1, o
 
         ts_listed = tile([P, N], F32, "ts_listed")
         nc.vector.tensor_copy(ts_listed[:], ts_window[:].indirect(offsets[:]))
-        ts_turned = bank([P, L, P])
+
+        ts_turned = bank(3, [P, L, P])
         for r in range(L):
             nc.tensor.transpose(ts_turned[:, r, :], ts_listed[:, r:N:L], ident[:])
         ts_cols = tile([P, L], F32, "ts_cols")
@@ -79,15 +84,15 @@ def tile_attend_gcau_pl_x_ts_kernel(tc, xT, wT, y, wt, ts, offs, out_0, out_1, o
 
         y_turned = [tile([P, L, P], F32, f"y_turned{j}") for j in range(L)]
 
-        def turn_y(j, lane, turned, copy):
+        def turn_y(j, b, copy):
+            turned = bank(b, [P, L, P])
             for r in range(L):
-                nc.tensor.transpose(turned[:, r, :], lane[:, r:N:L], ident[:])
+                nc.tensor.transpose(turned[:, r, :], y_lane[j][:, r:N:L], ident[:])
             copy(y_turned[j][:], turned[:])
 
-        for j in range(2):
-            turn_y(j, y_first[:, j * N:(j + 1) * N], bank([P, L, P]), nc.scalar.copy)
+        turn_y(0, 0, nc.scalar.copy)
 
-        wt_spread = bank([P, L, P])
+        wt_spread = bank(2, [P, L, P])
         for j in range(L):
             nc.tensor.transpose(wt_spread[:, j, :], wt_cols[:, j:j + 1].to_broadcast([P, P]), ident[:])
         coef = tile([P, L, L, P], F32, "coef")
@@ -96,67 +101,51 @@ def tile_attend_gcau_pl_x_ts_kernel(tc, xT, wT, y, wt, ts, offs, out_0, out_1, o
 
         wg = tile([P, N, L], BF16, "wg", tag="ts_window")
         wg_by_slot = wg[:].rearrange("p (r s) t -> p s r t", r=L)
-        wg_pairs = wg[:].rearrange("p c t -> p (c t)").bitcast(F32).rearrange("p (c u) -> p c u", u=2)
-        ws_codes = tile([P, D], U32, "ws_codes")
         ws_scales = tile([P, D], U8, "ws_scales")
 
         def gather_plane(t):
             nc.vector.tensor_copy(wg_by_slot[:, :, :, t], w_plane[t][:].indirect(offsets[:]))
 
-        def turn_pair(u):
-            turned = bank([P, L, P])
+        ws = tile([P, L, P, L], BF16, "ws")
+
+        def turn_plane(t, b):
+            turned = bank(b, [P, L, P], BF16)
             for r in range(L):
-                nc.tensor.transpose(turned[:, r, :], wg_pairs[:, r * P:(r + 1) * P, u], ident[:])
-            return turned
+                nc.tensor.transpose(turned[:, r, :], wg[:, r * P:(r + 1) * P, t], ident_bf[:])
+            nc.scalar.copy(ws[:, t], turned[:].rearrange("s r p -> s p r"))
 
-        def quantize_pair(u, turned, tag):
-            ws = tile([P, P, 2, L], BF16, f"ws{u}", tag=tag)
-            halves = turned[:].rearrange("s r p -> s (r p)").bitcast(BF16).rearrange("s (r p e) -> s p e r", r=L, e=2)
-            nc.scalar.copy(ws[:], halves)
-            cols = slice(u * D // 2, (u + 1) * D // 2)
-            nc.vector.quantize_mx(
-                out=ws_codes[:, cols].bitcast(E4), scales=ws_scales[:, cols], in_=ws[:].rearrange("s p e r -> s (p e r)"),
-            )
-
-        gather_plane(0)
-        x_raw = tile([P, L, R], F32, "x_raw", tag="w_plane0")
-        nc.sync.dma_start(x_raw[:], xT[0].rearrange("(p t) r -> p t r", t=L))
-        gather_plane(1)
-        y_lane2 = tile([P, N], F32, "y_lane2", tag="w_plane1")
-        nc.sync.dma_start(y_lane2[:], y_rows[:, 2 * N:3 * N])
-        quantize_pair(0, turn_pair(0), "ws0")
-        gather_plane(2)
-        y_lane3 = tile([P, N], F32, "y_lane3", tag="w_plane2")
-        nc.sync.dma_start(y_lane3[:], y_rows[:, 3 * N:])
-        gather_plane(3)
+        for t, b in enumerate((1, 0, 3, 2)):
+            gather_plane(t)
+            turn_plane(t, b)
         wg_codes = tile([P, N], U32, "wg_codes")
         wg_scales = tile([P, N], U8, "wg_scales")
         nc.vector.quantize_mx(out=wg_codes[:].bitcast(E4), scales=wg_scales[:], in_=wg[:].rearrange("p c t -> p (c t)"))
-        turned_pair = turn_pair(1)
 
-        xg = tile([P, L, P, L], BF16, "xg", tag="w_plane3")
-        xg_walk = xg[:].rearrange("p j m t -> p m t j")
         x_walk = x_raw[:].rearrange("p t (m j) -> p m t j", j=L)
-        nc.vector.tensor_copy(xg_walk[:, :X_ROWS_ON_VECTOR], x_walk[:, :X_ROWS_ON_VECTOR])
-        nc.scalar.copy(xg_walk[:, X_ROWS_ON_VECTOR:], x_walk[:, X_ROWS_ON_VECTOR:])
-        turn_y(2, y_lane2[:], bank([P, L, P]), nc.scalar.copy)
-        scores = []
-        for j in range(L):
-            x_codes = tile([P, P], U32, f"x_codes{j}")
-            x_scales = tile([P, P], U8, f"x_scales{j}")
+        x_codes = {}
+        x_scales = {}
+        for u, copy in enumerate((nc.vector.tensor_copy, nc.scalar.copy)):
+            xg = tile([P, 2, P, L], BF16, f"xg{u}")
+            copy(xg[:].rearrange("p j m t -> p m t j"), x_walk[:, :, :, 2 * u:2 * u + 2])
+            x_codes[u] = tile([P, 2 * P], U32, f"x_codes{u}")
+            x_scales[u] = tile([P, 2 * P], U8, f"x_scales{u}")
             nc.vector.quantize_mx(
-                out=x_codes[:].bitcast(E4), scales=x_scales[:], in_=xg[:, j, :, :].rearrange("p m t -> p (m t)"),
+                out=x_codes[u][:].bitcast(E4), scales=x_scales[u][:], in_=xg[:].rearrange("p j m t -> p (j m t)"),
             )
-            scores.append(ps_reused.tile([P, L, P], F32, name="reused") if j == 0 else bank([P, L, P]))
+        turn_y(1, 1, nc.scalar.copy)
+        scores = {}
+
+        def score(j):
+            scores[j] = bank(L + j, [P, L, P])
+            rows = slice(j % 2 * P, (j % 2 + 1) * P)
             for r in range(L):
+                slots = slice(r * P, (r + 1) * P)
                 nc.tensor.matmul_mx(
                     scores[j][:, r, :],
-                    lhsT=wg_codes[:, r * P:(r + 1) * P].bitcast(E4), lhsT_scale=wg_scales[:, r * P:(r + 1) * P],
-                    rhs=x_codes[:].bitcast(E4), rhs_scale=x_scales[:], start=True, stop=True,
+                    lhsT=wg_codes[:, slots].bitcast(E4), lhsT_scale=wg_scales[:, slots],
+                    rhs=x_codes[j // 2][:, rows].bitcast(E4), rhs_scale=x_scales[j // 2][:, rows], start=True, stop=True,
                 )
-        quantize_pair(1, turned_pair, "w_plane0")
 
-        result = tile([P, L, D], F32, "result")
         out_rows = out_0[0].rearrange("(m j) d -> m j d", j=L)
         q = [tile([P, L, P], F32, f"q{j}") for j in range(L)]
         qc = [tile([P, L, P], F32, f"qc{j}") for j in range(L)]
@@ -164,6 +153,8 @@ def tile_attend_gcau_pl_x_ts_kernel(tc, xT, wT, y, wt, ts, offs, out_0, out_1, o
         q_sq = [tile([P, L, P], F32, f"q_sq{j}") for j in range(L)]
         root = [tile([P, L, P], F32, f"root{j}") for j in range(L)]
         h = [tile([P, P, L], BF16, f"h{j}") for j in range(L)]
+        h_codes = [tile([P, P], U32, f"h_codes{j}") for j in range(L)]
+        h_scales = [tile([P, P], U8, f"h_scales{j}") for j in range(L)]
         acc = {}
 
         def residual(j):
@@ -175,36 +166,38 @@ def tile_attend_gcau_pl_x_ts_kernel(tc, xT, wT, y, wt, ts, offs, out_0, out_1, o
         def square(j):
             nc.scalar.activation(q_sq[j][:], q[j][:], ACT.Square)
 
-        def inverse_root(j):
-            nc.scalar.activation(root[j][:], q_sq[j][:], ACT.Abs_reciprocal_sqrt, bias=1.0)
+        def inverse_root(j, rows=slice(0, P)):
+            nc.scalar.activation(root[j][:, :, rows], q_sq[j][:, :, rows], ACT.Abs_reciprocal_sqrt, bias=1.0)
 
-        def damping(j):
-            nc.scalar.activation(damp[j][:], root[j][:], ACT.Square)
+        def damping(j, rows=slice(0, P)):
+            nc.scalar.activation(damp[j][:, :, rows], root[j][:, :, rows], ACT.Square)
 
         def weigh(j, engine):
             engine.tensor_tensor(qc[j][:], q[j][:], coef[:, j, :, :], ALU.mult)
 
-        def gradient(j):
+        def gradient(j, rows=slice(0, P)):
             nc.vector.tensor_tensor(
-                h[j][:].rearrange("s (c i) r -> s c r i", i=2),
-                qc[j][:].rearrange("s r (c i) -> s c r i", i=2),
-                damp[j][:].rearrange("s r (c i) -> s c r i", i=2),
+                h[j][:, rows].rearrange("s (c i) r -> s c r i", i=2),
+                qc[j][:, :, rows].rearrange("s r (c i) -> s c r i", i=2),
+                damp[j][:, :, rows].rearrange("s r (c i) -> s c r i", i=2),
                 ALU.mult,
             )
 
+        def quantize_h(j):
+            nc.vector.quantize_mx(
+                out=h_codes[j][:].bitcast(E5), scales=h_scales[j][:], in_=h[j][:].rearrange("s m r -> s (m r)"),
+            )
+
         def multiply(j):
-            h_codes = tile([P, P], U32, f"h_codes{j}")
-            h_scales = tile([P, P], U8, f"h_scales{j}")
-            nc.vector.quantize_mx(out=h_codes[:].bitcast(E5), scales=h_scales[:], in_=h[j][:].rearrange("s m r -> s (m r)"))
-            acc[j] = bank([P, D])
+            acc[j] = bank(j, [P, D])
             nc.tensor.matmul_mx(
-                acc[j][:], lhsT=h_codes[:].bitcast(E5), lhsT_scale=h_scales[:],
+                acc[j][:], lhsT=h_codes[j][:].bitcast(E5), lhsT_scale=h_scales[j][:],
                 rhs=ws_codes[:].bitcast(E4), rhs_scale=ws_scales[:], start=True, stop=True,
             )
 
         def emit(j, parts):
-            by_feature = acc[j][:].rearrange("m (u p e) -> m p u e", u=2, e=2)
-            dst = result[:, j, :].rearrange("m (p u e) -> m p u e", u=2, e=2)
+            by_feature = acc[j][:].rearrange("m (t p) -> m p t", t=L)
+            dst = result[:, j, :].rearrange("m (p t) -> m p t", t=L)
             step = P // parts
             for part in range(parts):
                 nc.scalar.copy(dst[:, part * step:(part + 1) * step], by_feature[:, part * step:(part + 1) * step])
@@ -221,35 +214,46 @@ def tile_attend_gcau_pl_x_ts_kernel(tc, xT, wT, y, wt, ts, offs, out_0, out_1, o
                 result[:, lanes, cols].rearrange("m j (c i) -> m c j i", i=4),
             )
 
-        for j in range(L - 1):
-            residual(j)
+        for j in range(L):
+            score(j)
+        residual(0)
+        residual(1)
         weigh(0, nc.gpsimd)
         weigh(1, nc.gpsimd)
-        turn_y(3, y_lane3[:], ps_reused.tile([P, L, P], F32, name="reused"), nc.vector.tensor_copy)
-
+        ws_codes = tile([P, D], U32, "ws_codes", tag="y_turned1")
+        nc.vector.quantize_mx(out=ws_codes[:].bitcast(E4), scales=ws_scales[:], in_=ws[:].rearrange("s t p r -> s (t p r)"))
+        turn_y(2, L, nc.vector.tensor_copy)
+        residual(2)
+        weigh(2, nc.gpsimd)
+        turn_y(3, L + 1, nc.vector.tensor_copy)
         residual(3)
+        row_halves = [slice(0, P // 2), slice(P // 2, P)]
         square(0)
         square(1)
         inverse_root(0)
-        square(2)
         inverse_root(1)
         damping(0)
-        inverse_root(2)
+        square(2)
         damping(1)
+        inverse_root(2)
         square(3)
         damping(2)
-        inverse_root(3)
-        damping(3)
+        for step in (inverse_root, damping):
+            for rows in row_halves:
+                step(3, rows)
         gradient(0)
-        weigh(2, nc.vector)
-        multiply(0)
-        gradient(1)
         weigh(3, nc.vector)
-        multiply(1)
+        quantize_h(0)
+        gradient(1)
+        quantize_h(1)
         gradient(2)
-        multiply(2)
-        gradient(3)
-        multiply(3)
+        quantize_h(2)
+        for rows in row_halves:
+            gradient(3, rows)
+        quantize_h(3)
+        result = tile([P, L, D], F32, "result", tag="root3")
+        for j in range(L):
+            multiply(j)
         for j in range(L - 1):
             emit(j, 1)
         weave(slice(0, 2), slice(0, D))

@@ -82,7 +82,10 @@ def tile_attend_gcau_pl_x_ts_kernel(tc, xT, wT, y, wt, ts, offs, out_0, out_1, o
         ts_cols = tile([P, L], F32, "ts_cols")
         nc.scalar.copy(ts_cols[:], ts_turned[:, :, 0])
 
-        y_turned = [tile([P, L, P], F32, f"y_turned{j}") for j in range(L)]
+        ts_negated = tile([P, L, P], F32, "ts_negated")
+        nc.scalar.activation(ts_negated[:], ts_listed[:].rearrange("q (s r) -> q r s", r=L), ACT.Copy, scale=-1.0)
+
+        y_turned = [tile([P, L, P], F32, f"y_turned{j}") for j in range(2)]
 
         def turn_y(j, b, copy):
             turned = bank(b, [P, L, P])
@@ -122,16 +125,21 @@ def tile_attend_gcau_pl_x_ts_kernel(tc, xT, wT, y, wt, ts, offs, out_0, out_1, o
         nc.vector.quantize_mx(out=wg_codes[:].bitcast(E4), scales=wg_scales[:], in_=wg[:].rearrange("p c t -> p (c t)"))
 
         x_walk = x_raw[:].rearrange("p t (m j) -> p m t j", j=L)
-        x_codes = {}
-        x_scales = {}
-        for u, copy in enumerate((nc.vector.tensor_copy, nc.scalar.copy)):
-            xg = tile([P, 2, P, L], BF16, f"xg{u}")
-            copy(xg[:].rearrange("p j m t -> p m t j"), x_walk[:, :, :, 2 * u:2 * u + 2])
-            x_codes[u] = tile([P, 2 * P], U32, f"x_codes{u}")
-            x_scales[u] = tile([P, 2 * P], U8, f"x_scales{u}")
+        xg = [tile([P, 2, P, L], BF16, f"xg{u}") for u in range(2)]
+        x_codes = [tile([P, 2 * P], U32, f"x_codes{u}") for u in range(2)]
+        x_scales = [tile([P, 2 * P], U8, f"x_scales{u}") for u in range(2)]
+
+        def quantize_x(u):
             nc.vector.quantize_mx(
-                out=x_codes[u][:].bitcast(E4), scales=x_scales[u][:], in_=xg[:].rearrange("p j m t -> p (j m t)"),
+                out=x_codes[u][:].bitcast(E4), scales=x_scales[u][:], in_=xg[u][:].rearrange("p j m t -> p (j m t)"),
             )
+
+        for u, copy in enumerate((nc.vector.tensor_copy, nc.scalar.copy)):
+            copy(xg[u][:].rearrange("p j m t -> p m t j"), x_walk[:, :, :, 2 * u:2 * u + 2])
+        quantize_x(0)
+        ws_codes = tile([P, D], U32, "ws_codes", tag="xg0")
+        nc.vector.quantize_mx(out=ws_codes[:].bitcast(E4), scales=ws_scales[:], in_=ws[:].rearrange("s t p r -> s (t p r)"))
+        quantize_x(1)
         turn_y(1, 1, nc.scalar.copy)
         scores = {}
 
@@ -146,8 +154,18 @@ def tile_attend_gcau_pl_x_ts_kernel(tc, xT, wT, y, wt, ts, offs, out_0, out_1, o
                     rhs=x_codes[j // 2][:, rows].bitcast(E4), rhs_scale=x_scales[j // 2][:, rows], start=True, stop=True,
                 )
 
+        def score_by_rows(j):
+            scores[j] = bank(L + j, [P, L, P])
+            rows = slice(j % 2 * P, (j % 2 + 1) * P)
+            nc.tensor.matmul_mx(
+                scores[j][:].rearrange("m r s -> m (r s)"),
+                lhsT=x_codes[j // 2][:, rows].bitcast(E4), lhsT_scale=x_scales[j // 2][:, rows],
+                rhs=wg_codes[:].bitcast(E4), rhs_scale=wg_scales[:], start=True, stop=True,
+            )
+
         out_rows = out_0[0].rearrange("(m j) d -> m j d", j=L)
-        q = [tile([P, L, P], F32, f"q{j}") for j in range(L)]
+        q = {j: tile([P, L, P], F32, f"q{j}") for j in range(2)}
+        scaled = {j: tile([P, L, P], F32, f"scaled{j}") for j in range(2, L)}
         qc = [tile([P, L, P], F32, f"qc{j}") for j in range(L)]
         damp = [tile([P, L, P], F32, f"damp{j}") for j in range(L)]
         q_sq = [tile([P, L, P], F32, f"q_sq{j}") for j in range(L)]
@@ -163,8 +181,24 @@ def tile_attend_gcau_pl_x_ts_kernel(tc, xT, wT, y, wt, ts, offs, out_0, out_1, o
                     q[j][:, r, :], scores[j][:, r, :], ts_cols[:, r:r + 1], y_turned[j][:, r, :], ALU.mult, ALU.subtract,
                 )
 
-        def square(j):
-            nc.scalar.activation(q_sq[j][:], q[j][:], ACT.Square)
+        def scale_scores(j):
+            nc.vector.tensor_tensor(scaled[j][:], scores[j][:], ts_negated[:], ALU.mult)
+
+        def residual_in_bank(j, b):
+            q[j] = bank(b, [P, L, P])
+            for r in range(L):
+                nc.tensor.matmul(q[j][:, r, :], y_lane[j][:, r:N:L], ident[:], is_transpose=True, start=r == 0, stop=False)
+            for r in range(L):
+                nc.tensor.matmul(q[j][:, r, :], scaled[j][:, r, :], ident[:], is_transpose=True, start=False, stop=r == L - 1)
+
+        def weigh_from_bank(j):
+            nc.vector.scalar_tensor_tensor(
+                qc[j][:].rearrange("s r m -> s (r m)"), q[j][:].rearrange("s r m -> s (r m)"), -1.0,
+                coef[:, j, :, :].rearrange("s r m -> s (r m)"), ALU.mult, ALU.mult,
+            )
+
+        def square(j, rows=slice(0, P)):
+            nc.scalar.activation(q_sq[j][:, :, rows], q[j][:, :, rows], ACT.Square)
 
         def inverse_root(j, rows=slice(0, P)):
             nc.scalar.activation(root[j][:, :, rows], q_sq[j][:, :, rows], ACT.Abs_reciprocal_sqrt, bias=1.0)
@@ -175,11 +209,11 @@ def tile_attend_gcau_pl_x_ts_kernel(tc, xT, wT, y, wt, ts, offs, out_0, out_1, o
         def weigh(j, engine):
             engine.tensor_tensor(qc[j][:], q[j][:], coef[:, j, :, :], ALU.mult)
 
-        def gradient(j, rows=slice(0, P)):
+        def gradient(j, first, second, rows=slice(0, P)):
             nc.vector.tensor_tensor(
                 h[j][:, rows].rearrange("s (c i) r -> s c r i", i=2),
-                qc[j][:, :, rows].rearrange("s r (c i) -> s c r i", i=2),
-                damp[j][:, :, rows].rearrange("s r (c i) -> s c r i", i=2),
+                first[:, :, rows].rearrange("s r (c i) -> s c r i", i=2),
+                second[:, :, rows].rearrange("s r (c i) -> s c r i", i=2),
                 ALU.mult,
             )
 
@@ -214,19 +248,19 @@ def tile_attend_gcau_pl_x_ts_kernel(tc, xT, wT, y, wt, ts, offs, out_0, out_1, o
                 result[:, lanes, cols].rearrange("m j (c i) -> m c j i", i=4),
             )
 
-        for j in range(L):
-            score(j)
+        score(0)
+        score(1)
+        score_by_rows(2)
+        score_by_rows(3)
         residual(0)
         residual(1)
         weigh(0, nc.gpsimd)
         weigh(1, nc.gpsimd)
-        ws_codes = tile([P, D], U32, "ws_codes", tag="y_turned1")
-        nc.vector.quantize_mx(out=ws_codes[:].bitcast(E4), scales=ws_scales[:], in_=ws[:].rearrange("s t p r -> s (t p r)"))
-        turn_y(2, L, nc.vector.tensor_copy)
-        residual(2)
-        weigh(2, nc.gpsimd)
-        turn_y(3, L + 1, nc.vector.tensor_copy)
-        residual(3)
+        scale_scores(2)
+        scale_scores(3)
+        residual_in_bank(2, L)
+        residual_in_bank(3, L + 1)
+        weigh_from_bank(2)
         row_halves = [slice(0, P // 2), slice(P // 2, P)]
         square(0)
         square(1)
@@ -236,20 +270,18 @@ def tile_attend_gcau_pl_x_ts_kernel(tc, xT, wT, y, wt, ts, offs, out_0, out_1, o
         square(2)
         damping(1)
         inverse_root(2)
-        square(3)
-        damping(2)
-        for step in (inverse_root, damping):
+        for step in (square, inverse_root, damping):
             for rows in row_halves:
                 step(3, rows)
-        gradient(0)
-        weigh(3, nc.vector)
-        quantize_h(0)
-        gradient(1)
-        quantize_h(1)
-        gradient(2)
+        for j in range(2):
+            gradient(j, qc[j], damp[j])
+            quantize_h(j)
+        nc.vector.tensor_tensor(damp[2][:], qc[2][:], root[2][:], ALU.mult)
+        weigh_from_bank(3)
+        gradient(2, damp[2], root[2])
         quantize_h(2)
         for rows in row_halves:
-            gradient(3, rows)
+            gradient(3, qc[3], damp[3], rows)
         quantize_h(3)
         result = tile([P, L, D], F32, "result", tag="root3")
         for j in range(L):

@@ -140,18 +140,24 @@ def tile_attend_gcau_pl_x_ts_kernel(tc, xT, wT, y, wt, ts, offs, out_0, out_1, o
         ws_codes = tile([P, D], U32, "ws_codes", tag="xg0")
         nc.vector.quantize_mx(out=ws_codes[:].bitcast(E4), scales=ws_scales[:], in_=ws[:].rearrange("s t p r -> s (t p r)"))
         quantize_x(1)
+        y_dealt = tile([P, 2, L, P], F32, "y_dealt", tag="xg1")
+        for j in range(2, L):
+            nc.gpsimd.tensor_scalar(
+                y_dealt[:, j - 2], y_lane[j][:].rearrange("m (s r) -> m r s", r=L), 1.0, 0.0, ALU.mult, ALU.add,
+            )
         turn_y(1, 1, nc.scalar.copy)
         scores = {}
 
-        def score(j):
-            scores[j] = bank(L + j, [P, L, P])
-            rows = slice(j % 2 * P, (j % 2 + 1) * P)
-            for r in range(L):
+        def score(j, b, places):
+            part = bank(b, [P, len(places), P])
+            rows = slice(j * P, (j + 1) * P)
+            for k, r in enumerate(places):
+                scores[j, r] = part[:, k, :]
                 slots = slice(r * P, (r + 1) * P)
                 nc.tensor.matmul_mx(
-                    scores[j][:, r, :],
+                    scores[j, r],
                     lhsT=wg_codes[:, slots].bitcast(E4), lhsT_scale=wg_scales[:, slots],
-                    rhs=x_codes[j // 2][:, rows].bitcast(E4), rhs_scale=x_scales[j // 2][:, rows], start=True, stop=True,
+                    rhs=x_codes[0][:, rows].bitcast(E4), rhs_scale=x_scales[0][:, rows], start=True, stop=True,
                 )
 
         def score_by_rows(j):
@@ -178,7 +184,7 @@ def tile_attend_gcau_pl_x_ts_kernel(tc, xT, wT, y, wt, ts, offs, out_0, out_1, o
         def residual(j):
             for r in range(L):
                 nc.vector.scalar_tensor_tensor(
-                    q[j][:, r, :], scores[j][:, r, :], ts_cols[:, r:r + 1], y_turned[j][:, r, :], ALU.mult, ALU.subtract,
+                    q[j][:, r, :], scores[j, r], ts_cols[:, r:r + 1], y_turned[j][:, r, :], ALU.mult, ALU.subtract,
                 )
 
         def scale_scores(j):
@@ -187,7 +193,7 @@ def tile_attend_gcau_pl_x_ts_kernel(tc, xT, wT, y, wt, ts, offs, out_0, out_1, o
         def residual_in_bank(j, b):
             q[j] = bank(b, [P, L, P])
             for r in range(L):
-                nc.tensor.matmul(q[j][:, r, :], y_lane[j][:, r:N:L], ident[:], is_transpose=True, start=r == 0, stop=False)
+                nc.tensor.matmul(q[j][:, r, :], y_dealt[:, j - 2, r, :], ident[:], is_transpose=True, start=r == 0, stop=False)
             for r in range(L):
                 nc.tensor.matmul(q[j][:, r, :], scaled[j][:, r, :], ident[:], is_transpose=True, start=False, stop=r == L - 1)
 
@@ -197,11 +203,11 @@ def tile_attend_gcau_pl_x_ts_kernel(tc, xT, wT, y, wt, ts, offs, out_0, out_1, o
                 coef[:, j, :, :].rearrange("s r m -> s (r m)"), ALU.mult, ALU.mult,
             )
 
-        def square(j, rows=slice(0, P)):
-            nc.scalar.activation(q_sq[j][:, :, rows], q[j][:, :, rows], ACT.Square)
+        def square(j, places=slice(0, L), rows=slice(0, P)):
+            nc.scalar.activation(q_sq[j][:, places, rows], q[j][:, places, rows], ACT.Square)
 
-        def inverse_root(j, rows=slice(0, P)):
-            nc.scalar.activation(root[j][:, :, rows], q_sq[j][:, :, rows], ACT.Abs_reciprocal_sqrt, bias=1.0)
+        def inverse_root(j, places=slice(0, L), rows=slice(0, P)):
+            nc.scalar.activation(root[j][:, places, rows], q_sq[j][:, places, rows], ACT.Abs_reciprocal_sqrt, bias=1.0)
 
         def damping(j, rows=slice(0, P)):
             nc.scalar.activation(damp[j][:, :, rows], root[j][:, :, rows], ACT.Square)
@@ -248,8 +254,9 @@ def tile_attend_gcau_pl_x_ts_kernel(tc, xT, wT, y, wt, ts, offs, out_0, out_1, o
                 result[:, lanes, cols].rearrange("m j (c i) -> m c j i", i=4),
             )
 
-        score(0)
-        score(1)
+        score(0, 0, (0, 1))
+        score(0, L, (2, 3))
+        score(1, L + 1, range(L))
         score_by_rows(2)
         score_by_rows(3)
         residual(0)
@@ -261,23 +268,24 @@ def tile_attend_gcau_pl_x_ts_kernel(tc, xT, wT, y, wt, ts, offs, out_0, out_1, o
         residual_in_bank(2, L)
         residual_in_bank(3, L + 1)
         weigh_from_bank(2)
+        weigh_from_bank(3)
         row_halves = [slice(0, P // 2), slice(P // 2, P)]
-        square(0)
+        for step in (square, inverse_root):
+            for places in (slice(0, 2), slice(2, L)):
+                step(0, places=places)
         square(1)
-        inverse_root(0)
-        inverse_root(1)
         damping(0)
+        inverse_root(1)
         square(2)
         damping(1)
         inverse_root(2)
         for step in (square, inverse_root, damping):
             for rows in row_halves:
-                step(3, rows)
+                step(3, rows=rows)
         for j in range(2):
             gradient(j, qc[j], damp[j])
             quantize_h(j)
         nc.vector.tensor_tensor(damp[2][:], qc[2][:], root[2][:], ALU.mult)
-        weigh_from_bank(3)
         gradient(2, damp[2], root[2])
         quantize_h(2)
         for rows in row_halves:

@@ -140,11 +140,6 @@ def tile_attend_gcau_pl_x_ts_kernel(tc, xT, wT, y, wt, ts, offs, out_0, out_1, o
         ws_codes = tile([P, D], U32, "ws_codes", tag="xg0")
         nc.vector.quantize_mx(out=ws_codes[:].bitcast(E4), scales=ws_scales[:], in_=ws[:].rearrange("s t p r -> s (t p r)"))
         quantize_x(1)
-        y_dealt = tile([P, 2, L, P], F32, "y_dealt", tag="xg1")
-        for j in range(2, L):
-            nc.gpsimd.tensor_scalar(
-                y_dealt[:, j - 2], y_lane[j][:].rearrange("m (s r) -> m r s", r=L), 1.0, 0.0, ALU.mult, ALU.add,
-            )
         turn_y(1, 1, nc.scalar.copy)
         scores = {}
 
@@ -193,7 +188,7 @@ def tile_attend_gcau_pl_x_ts_kernel(tc, xT, wT, y, wt, ts, offs, out_0, out_1, o
         def residual_in_bank(j, b):
             q[j] = bank(b, [P, L, P])
             for r in range(L):
-                nc.tensor.matmul(q[j][:, r, :], y_dealt[:, j - 2, r, :], ident[:], is_transpose=True, start=r == 0, stop=False)
+                nc.tensor.matmul(q[j][:, r, :], y_lane[j][:, r:N:L], ident[:], is_transpose=True, start=r == 0, stop=False)
             for r in range(L):
                 nc.tensor.matmul(q[j][:, r, :], scaled[j][:, r, :], ident[:], is_transpose=True, start=False, stop=r == L - 1)
 

@@ -136,7 +136,12 @@ def tile_attend_gcau_pl_x_ts_kernel(tc, xT, wT, y, wt, ts, offs, out_0, out_1, o
 
         for u, copy in enumerate((nc.vector.tensor_copy, nc.scalar.copy)):
             copy(xg[u][:].rearrange("p j m t -> p m t j"), x_walk[:, :, :, 2 * u:2 * u + 2])
-        quantize_x(0)
+        for j in range(2):
+            rows = slice(j * P, (j + 1) * P)
+            nc.vector.quantize_mx(
+                out=x_codes[0][:, rows].bitcast(E4), scales=x_scales[0][:, rows],
+                in_=xg[0][:, j].rearrange("p m t -> p (m t)"),
+            )
         ws_codes = tile([P, D], U32, "ws_codes", tag="xg0")
         nc.vector.quantize_mx(out=ws_codes[:].bitcast(E4), scales=ws_scales[:], in_=ws[:].rearrange("s t p r -> s (t p r)"))
         quantize_x(1)
@@ -285,7 +290,11 @@ def tile_attend_gcau_pl_x_ts_kernel(tc, xT, wT, y, wt, ts, offs, out_0, out_1, o
         quantize_h(2)
         for rows in row_halves:
             gradient(3, qc[3], damp[3], rows)
-        quantize_h(3)
+        for rows in row_halves:
+            nc.vector.quantize_mx(
+                out=h_codes[3][:, rows].bitcast(E5), scales=h_scales[3][:, rows],
+                in_=h[3][:, rows].rearrange("s m r -> s (m r)"),
+            )
         result = tile([P, L, D], F32, "result", tag="root3")
         for j in range(L):
             multiply(j)

@@ -109,13 +109,13 @@ def tile_attend_gcau_pl_x_ts_kernel(tc, xT, wT, y, wt, ts, offs, out_0, out_1, o
         def gather_plane(t):
             nc.vector.tensor_copy(wg_by_slot[:, :, :, t], w_plane[t][:].indirect(offsets[:]))
 
-        ws = tile([P, L, P, L], BF16, "ws")
+        ws = tile([P, 2, L, P // 2, L], BF16, "ws")
 
         def turn_plane(t, b):
             turned = bank(b, [P, L, P], BF16)
             for r in range(L):
                 nc.tensor.transpose(turned[:, r, :], wg[:, r * P:(r + 1) * P, t], ident_bf[:])
-            nc.scalar.copy(ws[:, t], turned[:].rearrange("s r p -> s p r"))
+            nc.scalar.copy(ws[:, :, t], turned[:].rearrange("s r (u p) -> s u p r", u=2))
 
         for t, b in enumerate((1, 0, 3, 2)):
             gather_plane(t)
@@ -143,7 +143,7 @@ def tile_attend_gcau_pl_x_ts_kernel(tc, xT, wT, y, wt, ts, offs, out_0, out_1, o
                 in_=xg[0][:, j].rearrange("p m t -> p (m t)"),
             )
         ws_codes = tile([P, D], U32, "ws_codes", tag="xg0")
-        nc.vector.quantize_mx(out=ws_codes[:].bitcast(E4), scales=ws_scales[:], in_=ws[:].rearrange("s t p r -> s (t p r)"))
+        nc.vector.quantize_mx(out=ws_codes[:].bitcast(E4), scales=ws_scales[:], in_=ws[:].rearrange("s u t p r -> s (u t p r)"))
         quantize_x(1)
         turn_y(1, 1, nc.scalar.copy)
         scores = {}
@@ -228,20 +228,18 @@ def tile_attend_gcau_pl_x_ts_kernel(tc, xT, wT, y, wt, ts, offs, out_0, out_1, o
                 out=h_codes[j][:].bitcast(E5), scales=h_scales[j][:], in_=h[j][:].rearrange("s m r -> s (m r)"),
             )
 
-        def multiply(j):
-            acc[j] = bank(j, [P, D])
+        def multiply(j, b, cols):
+            acc[j, cols.start] = bank(b, [P, cols.stop - cols.start])
             nc.tensor.matmul_mx(
-                acc[j][:], lhsT=h_codes[j][:].bitcast(E5), lhsT_scale=h_scales[j][:],
-                rhs=ws_codes[:].bitcast(E4), rhs_scale=ws_scales[:], start=True, stop=True,
+                acc[j, cols.start][:], lhsT=h_codes[j][:].bitcast(E5), lhsT_scale=h_scales[j][:],
+                rhs=ws_codes[:, cols].bitcast(E4), rhs_scale=ws_scales[:, cols], start=True, stop=True,
             )
 
-        def emit(j, parts):
-            by_feature = acc[j][:].rearrange("m (t p) -> m p t", t=L)
-            dst = result[:, j, :].rearrange("m (p t) -> m p t", t=L)
-            step = P // parts
-            for part in range(parts):
-                nc.scalar.copy(dst[:, part * step:(part + 1) * step], by_feature[:, part * step:(part + 1) * step])
-            nc.sync.dma_start(out_rows[:, j, :], result[:, j, :])
+        def emit(j, cols):
+            nc.scalar.copy(
+                result[:, j, cols].rearrange("m (u p t) -> m u p t", p=P // 2, t=L),
+                acc[j, cols.start][:].rearrange("m (u t p) -> m u p t", p=P // 2, t=L),
+            )
 
         planes = tile([P, D, L], BF16, "planes")
         out_codes = tile([P, D], U32, "out_codes")
@@ -296,13 +294,19 @@ def tile_attend_gcau_pl_x_ts_kernel(tc, xT, wT, y, wt, ts, offs, out_0, out_1, o
                 in_=h[3][:, rows].rearrange("s m r -> s (m r)"),
             )
         result = tile([P, L, D], F32, "result", tag="root3")
-        for j in range(L):
-            multiply(j)
-        for j in range(L - 1):
-            emit(j, 1)
-        weave(slice(0, 2), slice(0, D))
-        emit(3, 2)
+        whole = slice(0, D)
         halves = [slice(0, D // 2), slice(D // 2, D)]
+        for j in range(L - 1):
+            multiply(j, j, whole)
+        for b, cols in zip((3, 7), halves):
+            multiply(3, b, cols)
+        for j in range(L - 1):
+            emit(j, whole)
+            nc.sync.dma_start(out_rows[:, j, :], result[:, j, :])
+        weave(slice(0, 2), whole)
+        for cols in halves:
+            emit(3, cols)
+        nc.sync.dma_start(out_rows[:, 3, :], result[:, 3, :])
         for cols in halves:
             weave(slice(2, 4), cols)
         for cols in halves:

@@ -275,7 +275,8 @@ def tile_attend_gcau_pl_x_ts_kernel(tc, xT, wT, y, wt, ts, offs, out_0, out_1, o
         damping(0)
         inverse_root(1)
         square(2)
-        damping(1)
+        nc.scalar.activation(damp[1][:, 0:2], root[1][:, 0:2], ACT.Square)
+        nc.gpsimd.tensor_tensor(damp[1][:, 2:L], root[1][:, 2:L], root[1][:, 2:L], ALU.mult)
         inverse_root(2)
         for step in (square, inverse_root, damping):
             for rows in row_halves:

@@ -73,17 +73,14 @@ def tile_attend_gcau_pl_x_ts_kernel(tc, xT, wT, y, wt, ts, offs, out_0, out_1, o
             copy = nc.vector.tensor_copy if g % 2 else nc.scalar.copy
             copy(ts_by_run[:, :, L * g:L * g + L], spread[:].rearrange("q c p -> q p c"))
 
-        ts_listed = tile([P, N], F32, "ts_listed")
-        nc.vector.tensor_copy(ts_listed[:], ts_window[:].indirect(offsets[:]))
+        ts_dealt = tile([P, L, P], F32, "ts_dealt")
+        nc.vector.tensor_copy(ts_dealt[:].rearrange("q r s -> q s r"), ts_window[:].indirect(offsets[:]))
 
         ts_turned = bank(3, [P, L, P])
         for r in range(L):
-            nc.tensor.transpose(ts_turned[:, r, :], ts_listed[:, r:N:L], ident[:])
+            nc.tensor.transpose(ts_turned[:, r, :], ts_dealt[:, r, :], ident[:])
         ts_cols = tile([P, L], F32, "ts_cols")
         nc.scalar.copy(ts_cols[:], ts_turned[:, :, 0])
-
-        ts_negated = tile([P, L, P], F32, "ts_negated")
-        nc.scalar.activation(ts_negated[:], ts_listed[:].rearrange("q (s r) -> q r s", r=L), ACT.Copy, scale=-1.0)
 
         y_turned = [tile([P, L, P], F32, f"y_turned{j}") for j in range(2)]
 
@@ -188,7 +185,10 @@ def tile_attend_gcau_pl_x_ts_kernel(tc, xT, wT, y, wt, ts, offs, out_0, out_1, o
                 )
 
         def scale_scores(j):
-            nc.vector.tensor_tensor(scaled[j][:], scores[j][:], ts_negated[:], ALU.mult)
+            nc.vector.scalar_tensor_tensor(
+                scaled[j][:].rearrange("m r s -> m (r s)"), scores[j][:].rearrange("m r s -> m (r s)"), -1.0,
+                ts_dealt[:].rearrange("m r s -> m (r s)"), ALU.mult, ALU.mult,
+            )
 
         def residual_in_bank(j, b):
             q[j] = bank(b, [P, L, P])

@@ -217,9 +217,9 @@ def tile_attend_gcau_pl_x_ts_kernel(tc, xT, wT, y, wt, ts, offs, out_0, out_1, o
 
         def gradient(j, first, second, rows=slice(0, P)):
             nc.vector.tensor_tensor(
-                h[j][:, rows].rearrange("s (c i) r -> s c r i", i=2),
-                first[:, :, rows].rearrange("s r (c i) -> s c r i", i=2),
-                second[:, :, rows].rearrange("s r (c i) -> s c r i", i=2),
+                h[j][:, rows].rearrange("s (c i) r -> s c r i", i=4),
+                first[:, :, rows].rearrange("s r (c i) -> s c r i", i=4),
+                second[:, :, rows].rearrange("s r (c i) -> s c r i", i=4),
                 ALU.mult,
             )
 

from contextlib import ExitStack

import concourse.mybir as mybir
from concourse.masks import make_identity

N, T, D, R = 512, 2048, 512, 512
P = 128
L = 4

FLOPS = 2 * 2 * R * N * D
BYTES = 4 * (D * R + D * T + R * N + R + T) + 2 * P * N // 16 + 4 * R * D + R * D + R * D // 32

F32 = mybir.dt.float32
BF16 = mybir.dt.bfloat16
U32 = mybir.dt.uint32
I32 = mybir.dt.int32
U16 = mybir.dt.uint16
U8 = mybir.dt.uint8
E4 = mybir.dt.float8_e4m3fn_x4
E5 = mybir.dt.float8_e5m2_x4
ALU = mybir.AluOpType
ACT = mybir.ActivationFunctionType


def tile_attend_gcau_pl_x_ts_kernel(tc, xT, wT, y, wt, ts, offs, out_0, out_1, out_2):
    nc = tc.nc
    with ExitStack() as ctx:
        lists = ctx.enter_context(tc.tile_pool(name="lists", bufs=1))
        sb = ctx.enter_context(tc.tile_pool(name="sb", bufs=1))
        ps = ctx.enter_context(tc.psum_pool(name="ps", bufs=1))

        def tile(shape, dtype, name, tag=None):
            return sb.tile(shape, dtype, name=name, tag=tag or name, align_bytes=64)

        def bank(b, shape, dtype=F32):
            return ps.tile(shape, dtype, name=f"bank{b}", tag=f"bank{b}")

        y_rows = y[0].rearrange("(m j) i -> m j i", j=L)
        w_rows = wT.rearrange("(p t) c -> p t c", t=L)

        offsets = lists.tile([P, N // 16], U16, name="offsets")
        wt_cols = tile([P, L], F32, "wt_cols")
        ts_runs = tile([P, T // P], F32, "ts_runs")
        x_raw = tile([P, L, R], F32, "x_raw")
        y_lane = [tile([P, N], F32, f"y_lane{j}") for j in range(L)]
        w_plane = [tile([P, T], F32, f"w_plane{t}") for t in range(L)]
        nc.sync.dma_start(ts_runs[:], ts[0].rearrange("(p c) -> p c", p=P))
        nc.sync.dma_start(y_lane[0][:], y_rows[:, 0, :])
        nc.sync.dma_start(offsets[:], offs)
        nc.sync.dma_start(wt_cols[:], wt[0].rearrange("(m j) o -> m (j o)", j=L))
        for t in range(L):
            nc.sync.dma_start(w_plane[t][:], w_rows[:, t, :])
        nc.sync.dma_start(x_raw[:], xT[0].rearrange("(p t) r -> p t r", t=L))
        for j in range(1, L):
            nc.sync.dma_start(y_lane[j][:], y_rows[:, j, :])

        warm_in = tile([P, 1], F32, "warm_in")
        warm_out = tile([P, 1], F32, "warm_out")
        nc.vector.memset(warm_in[:], 1.0)
        nc.scalar.activation(warm_out[:], warm_in[:], ACT.Abs_reciprocal_sqrt)

        ident = tile([P, P], F32, "ident")
        make_identity(nc, ident[:])
        ident_bf = tile([P, P], BF16, "ident_bf")
        make_identity(nc, ident_bf[:])

        ts_window = tile([P, T], F32, "ts_window")
        ts_by_run = ts_window[:].rearrange("q (p c) -> q p c", p=P)
        for g in range(T // P // L):
            spread = bank(g, [P, L, P])
            for c in range(L):
                nc.tensor.transpose(spread[:, c, :], ts_runs[:, L * g + c:L * g + c + 1].to_broadcast([P, P]), ident[:])
            copy = nc.vector.tensor_copy if g % 2 else nc.scalar.copy
            copy(ts_by_run[:, :, L * g:L * g + L], spread[:].rearrange("q c p -> q p c"))

        ts_dealt = tile([P, L, P], F32, "ts_dealt")
        nc.vector.tensor_copy(ts_dealt[:].rearrange("q r s -> q s r"), ts_window[:].indirect(offsets[:]))

        ts_turned = bank(3, [P, L, P])
        for r in range(L):
            nc.tensor.transpose(ts_turned[:, r, :], ts_dealt[:, r, :], ident[:])
        ts_cols = tile([P, L], F32, "ts_cols")
        nc.scalar.copy(ts_cols[:], ts_turned[:, :, 0])

        y_turned = [tile([P, L, P], F32, f"y_turned{j}") for j in range(2)]

        def turn_y(j, b, copy):
            turned = bank(b, [P, L, P])
            for r in range(L):
                nc.tensor.transpose(turned[:, r, :], y_lane[j][:, r:N:L], ident[:])
            copy(y_turned[j][:], turned[:])

        turn_y(0, 0, nc.scalar.copy)

        wt_spread = bank(2, [P, L, P])
        for j in range(L):
            nc.tensor.transpose(wt_spread[:, j, :], wt_cols[:, j:j + 1].to_broadcast([P, P]), ident[:])
        coef = tile([P, L, L, P], F32, "coef")
        for r in range(L):
            nc.scalar.activation(coef[:, :, r, :], wt_spread[:], ACT.Copy, scale=ts_cols[:, r:r + 1])

        wg = tile([P, N, L], BF16, "wg", tag="ts_window")
        wg_by_slot = wg[:].rearrange("p (r s) t -> p s r t", r=L)
        ws_scales = tile([P, D], U8, "ws_scales")

        def gather_plane(t):
            nc.vector.tensor_copy(wg_by_slot[:, :, :, t], w_plane[t][:].indirect(offsets[:]))

        ws = tile([P, 2, L, P // 2, L], BF16, "ws")

        def turn_plane(t, b):
            turned = bank(b, [P, L, P], BF16)
            for r in range(L):
                nc.tensor.transpose(turned[:, r, :], wg[:, r * P:(r + 1) * P, t], ident_bf[:])
            nc.scalar.copy(ws[:, :, t], turned[:].rearrange("s r (u p) -> s u p r", u=2))

        for t, b in enumerate((1, 0, 3, 2)):
            gather_plane(t)
            turn_plane(t, b)
        wg_codes = tile([P, N], U32, "wg_codes")
        wg_scales = tile([P, N], U8, "wg_scales")
        nc.vector.quantize_mx(out=wg_codes[:].bitcast(E4), scales=wg_scales[:], in_=wg[:].rearrange("p c t -> p (c t)"))

        x_walk = x_raw[:].rearrange("p t (m j) -> p m t j", j=L)
        xg = [tile([P, 2, P, L], BF16, f"xg{u}") for u in range(2)]
        x_codes = [tile([P, 2 * P], U32, f"x_codes{u}") for u in range(2)]
        x_scales = [tile([P, 2 * P], U8, f"x_scales{u}") for u in range(2)]

        def quantize_x(u):
            nc.vector.quantize_mx(
                out=x_codes[u][:].bitcast(E4), scales=x_scales[u][:], in_=xg[u][:].rearrange("p j m t -> p (j m t)"),
            )

        for u, copy in enumerate((nc.vector.tensor_copy, nc.scalar.copy)):
            copy(xg[u][:].rearrange("p j m t -> p m t j"), x_walk[:, :, :, 2 * u:2 * u + 2])
        for j in range(2):
            rows = slice(j * P, (j + 1) * P)
            nc.vector.quantize_mx(
                out=x_codes[0][:, rows].bitcast(E4), scales=x_scales[0][:, rows],
                in_=xg[0][:, j].rearrange("p m t -> p (m t)"),
            )
        ws_codes = tile([P, D], U32, "ws_codes", tag="xg0")
        nc.vector.quantize_mx(out=ws_codes[:].bitcast(E4), scales=ws_scales[:], in_=ws[:].rearrange("s u t p r -> s (u t p r)"))
        quantize_x(1)
        turn_y(1, 1, nc.scalar.copy)
        scores = {}

        def score(j, b, places):
            part = bank(b, [P, len(places), P])
            rows = slice(j * P, (j + 1) * P)
            for k, r in enumerate(places):
                scores[j, r] = part[:, k, :]
                slots = slice(r * P, (r + 1) * P)
                nc.tensor.matmul_mx(
                    scores[j, r],
                    lhsT=wg_codes[:, slots].bitcast(E4), lhsT_scale=wg_scales[:, slots],
                    rhs=x_codes[0][:, rows].bitcast(E4), rhs_scale=x_scales[0][:, rows], start=True, stop=True,
                )

        def score_by_rows(j):
            scores[j] = bank(L + j, [P, L, P])
            rows = slice(j % 2 * P, (j % 2 + 1) * P)
            nc.tensor.matmul_mx(
                scores[j][:].rearrange("m r s -> m (r s)"),
                lhsT=x_codes[j // 2][:, rows].bitcast(E4), lhsT_scale=x_scales[j // 2][:, rows],
                rhs=wg_codes[:].bitcast(E4), rhs_scale=wg_scales[:], start=True, stop=True,
            )

        out_rows = out_0[0].rearrange("(m j) d -> m j d", j=L)
        q = {j: tile([P, L, P], F32, f"q{j}") for j in range(2)}
        scaled = {j: tile([P, L, P], F32, f"scaled{j}") for j in range(2, L)}
        qc = [tile([P, L, P], F32, f"qc{j}") for j in range(L)]
        damp = [tile([P, L, P], F32, f"damp{j}") for j in range(L)]
        q_sq = [tile([P, L, P], F32, f"q_sq{j}") for j in range(L)]
        root = [tile([P, L, P], F32, f"root{j}") for j in range(L)]
        h = [tile([P, P, L], BF16, f"h{j}") for j in range(L)]
        h_codes = [tile([P, P], U32, f"h_codes{j}") for j in range(L)]
        h_scales = [tile([P, P], U8, f"h_scales{j}") for j in range(L)]
        acc = {}

        def residual(j):
            for r in range(L):
                nc.vector.scalar_tensor_tensor(
                    q[j][:, r, :], scores[j, r], ts_cols[:, r:r + 1], y_turned[j][:, r, :], ALU.mult, ALU.subtract,
                )

        def scale_scores(j):
            nc.vector.scalar_tensor_tensor(
                scaled[j][:].rearrange("m r s -> m (r s)"), scores[j][:].rearrange("m r s -> m (r s)"), -1.0,
                ts_dealt[:].rearrange("m r s -> m (r s)"), ALU.mult, ALU.mult,
            )

        def residual_in_bank(j, b):
            q[j] = bank(b, [P, L, P])
            for r in range(L):
                nc.tensor.matmul(q[j][:, r, :], y_lane[j][:, r:N:L], ident[:], is_transpose=True, start=r == 0, stop=False)
            for r in range(L):
                nc.tensor.matmul(q[j][:, r, :], scaled[j][:, r, :], ident[:], is_transpose=True, start=False, stop=r == L - 1)

        def weigh_from_bank(j):
            nc.vector.scalar_tensor_tensor(
                qc[j][:].rearrange("s r m -> s (r m)"), q[j][:].rearrange("s r m -> s (r m)"), -1.0,
                coef[:, j, :, :].rearrange("s r m -> s (r m)"), ALU.mult, ALU.mult,
            )

        def square(j, places=slice(0, L), rows=slice(0, P)):
            nc.scalar.activation(q_sq[j][:, places, rows], q[j][:, places, rows], ACT.Square)

        def inverse_root(j, places=slice(0, L), rows=slice(0, P)):
            nc.scalar.activation(root[j][:, places, rows], q_sq[j][:, places, rows], ACT.Abs_reciprocal_sqrt, bias=1.0)

        def damping(j, rows=slice(0, P)):
            nc.scalar.activation(damp[j][:, :, rows], root[j][:, :, rows], ACT.Square)

        def weigh(j, engine):
            engine.tensor_tensor(qc[j][:], q[j][:], coef[:, j, :, :], ALU.mult)

        def gradient(j, first, second, rows=slice(0, P)):
            nc.vector.tensor_tensor(
                h[j][:, rows].rearrange("s (c i) r -> s c r i", i=4),
                first[:, :, rows].rearrange("s r (c i) -> s c r i", i=4),
                second[:, :, rows].rearrange("s r (c i) -> s c r i", i=4),
                ALU.mult,
            )

        def quantize_h(j):
            nc.vector.quantize_mx(
                out=h_codes[j][:].bitcast(E5), scales=h_scales[j][:], in_=h[j][:].rearrange("s m r -> s (m r)"),
            )

        def multiply(j, b, cols):
            acc[j, cols.start] = bank(b, [P, cols.stop - cols.start])
            nc.tensor.matmul_mx(
                acc[j, cols.start][:], lhsT=h_codes[j][:].bitcast(E5), lhsT_scale=h_scales[j][:],
                rhs=ws_codes[:, cols].bitcast(E4), rhs_scale=ws_scales[:, cols], start=True, stop=True,
            )

        def emit(j, cols):
            nc.scalar.copy(
                result[:, j, cols].rearrange("m (u p t) -> m u p t", p=P // 2, t=L),
                acc[j, cols.start][:].rearrange("m (u t p) -> m u p t", p=P // 2, t=L),
            )

        planes = tile([P, D, L], BF16, "planes")
        out_codes = tile([P, D], U32, "out_codes")
        out_scales = tile([P, D], U8, "out_scales")
        words = out_1[0].rearrange("m d j -> m (d j)").bitcast(I32)

        def weave(lanes, cols):
            nc.vector.tensor_copy(
                planes[:, cols, lanes].rearrange("m (c i) j -> m c j i", i=4),
                result[:, lanes, cols].rearrange("m j (c i) -> m c j i", i=4),
            )

        score(0, 0, (0, 1))
        score(0, L, (2, 3))
        score(1, L + 1, range(L))
        score_by_rows(2)
        score_by_rows(3)
        residual(0)
        residual(1)
        weigh(0, nc.gpsimd)
        weigh(1, nc.gpsimd)
        scale_scores(2)
        scale_scores(3)
        residual_in_bank(2, L)
        residual_in_bank(3, L + 1)
        weigh_from_bank(2)
        weigh_from_bank(3)
        row_halves = [slice(0, P // 2), slice(P // 2, P)]
        for step in (square, inverse_root):
            for places in (slice(0, 2), slice(2, L)):
                step(0, places=places)
        square(1)
        damping(0)
        inverse_root(1)
        square(2)
        nc.scalar.activation(damp[1][:, 0:2], root[1][:, 0:2], ACT.Square)
        nc.gpsimd.tensor_tensor(damp[1][:, 2:L], root[1][:, 2:L], root[1][:, 2:L], ALU.mult)
        inverse_root(2)
        for step in (square, inverse_root, damping):
            for rows in row_halves:
                step(3, rows=rows)
        for j in range(2):
            gradient(j, qc[j], damp[j])
            quantize_h(j)
        nc.vector.tensor_tensor(damp[2][:], qc[2][:], root[2][:], ALU.mult)
        gradient(2, damp[2], root[2])
        quantize_h(2)
        for rows in row_halves:
            gradient(3, qc[3], damp[3], rows)
        for rows in row_halves:
            nc.vector.quantize_mx(
                out=h_codes[3][:, rows].bitcast(E5), scales=h_scales[3][:, rows],
                in_=h[3][:, rows].rearrange("s m r -> s (m r)"),
            )
        result = tile([P, L, D], F32, "result", tag="root3")
        whole = slice(0, D)
        halves = [slice(0, D // 2), slice(D // 2, D)]
        for j in range(L - 1):
            multiply(j, j, whole)
        for b, cols in zip((3, 7), halves):
            multiply(3, b, cols)
        for j in range(L - 1):
            emit(j, whole)
            nc.sync.dma_start(out_rows[:, j, :], result[:, j, :])
        weave(slice(0, 2), whole)
        for cols in halves:
            emit(3, cols)
        nc.sync.dma_start(out_rows[:, 3, :], result[:, 3, :])
        for cols in halves:
            weave(slice(2, 4), cols)
        for cols in halves:
            nc.vector.quantize_mx(
                out=out_codes[:, cols].bitcast(E4), scales=out_scales[:, cols],
                in_=planes[:, cols, :].rearrange("m d j -> m (d j)"),
            )
            nc.sync.dma_start(words[:, cols], out_codes[:, cols].bitcast(I32))
        for quad in range(4):
            eng = nc.scalar if quad % 2 else nc.sync
            eng.dma_start(out_2[0, 4 * quad:4 * quad + 4, :].bitcast(I32), out_scales[32 * quad:32 * quad + 4, :].bitcast(I32))
